import numpy as np
import ml_dtypes


def mxq(x, axis, fmt="e4m3"):
    dtype, down = {"e4m3": (ml_dtypes.float8_e4m3fn, 7), "e5m2": (ml_dtypes.float8_e5m2, 14)}[fmt]
    v = np.moveaxis(np.asarray(x, np.float32).astype(ml_dtypes.bfloat16).astype(np.float64), axis, -1)
    blocks = v.reshape(v.shape[:-1] + (-1, 32))
    amax = np.abs(blocks).max(-1, keepdims=True)
    byte = np.maximum(np.where(amax > 0, np.frexp(amax)[1] - 1 + 127, 0) - down, 1)
    scale = np.exp2(byte - 127.0)
    codes = (blocks / scale).astype(np.float32).astype(dtype).astype(np.float64)
    return np.moveaxis((codes * scale).reshape(v.shape), -1, axis)


WIDE = False


def mx_kscale(k):
    if not WIDE:
        return np.ones(k)
    levels = np.array([10, -10, 5, -5, 0])
    if k % 512:
        return np.exp2(np.random.permutation(np.resize(levels, k // 32))).repeat(32)
    a = np.empty((k // 512, 16))
    for p in range(k // 512):
        a[p, :8] = np.random.permutation(np.resize(levels, 8))
        for g in range(8):
            far = levels[np.abs(levels - a[p, g]) >= 10]
            a[p, g + 8] = far[np.random.randint(len(far))]
    return np.exp2(a.ravel()).repeat(32)


def f64(x):
    return np.asarray(x).astype(np.float64)


def striped(idx):
    return np.tile(np.asarray(idx).reshape(-1, 16).T, (8, 1)).astype(np.uint16)


def unstriped(offs):
    return offs[:16].T.reshape(-1).astype(np.int64)


E2M1 = np.array([0.0, 0.5, 1.0, 1.5, 2.0, 3.0, 4.0, 6.0, -0.0, -0.5, -1.0, -1.5, -2.0, -3.0, -4.0, -6.0])


def pack_weight(w, fmt):
    k, n = w.shape
    w = f64(np.asarray(w, np.float32).astype(ml_dtypes.bfloat16)).reshape(k // 32, 32, n)
    amax = np.abs(w).max(1)
    if fmt == "e4m3":
        byte = np.frexp(amax)[1] - 1 + 127 - 7
    else:
        mant, ex = np.frexp(amax / 6.0)
        byte = np.where(mant > 0.5, ex, ex - 1) + 127
    byte = np.clip(np.where(amax > 0, byte, 1), 1, 254)
    scaled = (w * np.exp2(127.0 - byte)[:, None, :]).reshape(k, n).astype(np.float32)
    by_word = np.ascontiguousarray(scaled.reshape(k // 512, 128, 4, n).transpose(0, 1, 3, 2))
    if fmt == "e4m3":
        words = by_word.astype(ml_dtypes.float8_e4m3fn).view(np.uint8)
    else:
        c = by_word.astype(ml_dtypes.float4_e2m1fn).view(np.uint8) & 0xF
        words = (c[..., 0::2] | (c[..., 1::2] << 4)).reshape(k // 512, 128, 2 * n)
    return np.ascontiguousarray(words), np.ascontiguousarray(byte.astype(np.uint8).reshape(k // 512, 16, n))


def unpack_weight(words, scales, fmt):
    g, _, n = scales.shape
    words = np.ascontiguousarray(words).reshape(g, 128, n, -1)
    if fmt == "e4m3":
        vals = words.view(ml_dtypes.float8_e4m3fn).astype(np.float64)
    else:
        nib = np.empty((g, 128, n, 4), np.uint8)
        nib[..., 0::2] = words & 0xF
        nib[..., 1::2] = words >> 4
        vals = E2M1[nib]
    vals = vals * np.repeat(np.exp2(scales.astype(np.float64) - 127.0), 8, axis=1)[..., None]
    return vals.transpose(0, 1, 3, 2).reshape(g * 512, n)


B, N, T, D, NQ = 1, 512, 2048, 1024, 512
DV = 512


def sgn(shape):
    return np.random.uniform(0.5, 2.0, shape) * np.where(np.random.standard_normal(shape) < 0, -1.0, 1.0)


def setup_inputs():
    n = np.random.standard_normal
    idx = np.random.permutation(T)[:B * N]
    s = mx_kscale(D)[:, None]
    u = mx_kscale(N)
    ut = np.ones(T)
    ut[idx] = u
    kp = pack_weight(n((D, T)) / s, "e2m1")
    return {
        "qT": (n((B, D, NQ)) * s * (1.00 / np.sqrt(D))).astype(np.float32),
        "k_words": np.ascontiguousarray(kp[0].reshape(1, 2, 128, T, 2).transpose(0, 2, 3, 1, 4)).reshape(1, 128, T, 4),
        "k_scales": kp[1],
        "vT": (n((DV, T)) / ut).astype(np.float32),
        "ts": np.tile(np.random.uniform(0.5, 2.0, 2048), (128, 1)).astype(np.float32),
        "us": (sgn((B, N, 1)) * u[:, None]).astype(np.float32),
        "offs": striped(idx),
    }


def reference(qT, k_words, k_scales, vT, ts, us, offs):
    idx = unstriped(offs)
    pick = lambda x, which: x[:, which].reshape(x.shape[0], B, -1).transpose(1, 0, 2)
    k = unpack_weight(k_words.reshape(1, 128, T, 2, 2).transpose(0, 3, 1, 2, 4).reshape(2, 128, 2 * T), k_scales, "e2m1")
    kg = pick(k, idx)
    qq = mxq(f64(qT), 1, "e4m3")
    a = kg.transpose(0, 2, 1) @ qq
    y = np.square(np.maximum(a * pick(f64(ts), idx)[:, :1, :].transpose(0, 2, 1), 0.0)) * f64(us)
    wq = mxq(y, 1, "e4m3")
    o = wq.transpose(0, 2, 1) @ mxq(pick(f64(vT), idx).transpose(0, 2, 1), 1, "e4m3")
    ms = np.mean(np.square(o), axis=-1, keepdims=True)
    r_ = o / np.sqrt(ms + 1e-05)
    return r_

@@ -1,0 +1,260 @@
+from contextlib import ExitStack
+
+import concourse.mybir as mybir
+from concourse.masks import make_identity
+
+F32 = mybir.dt.float32
+BF16 = mybir.dt.bfloat16
+I32 = mybir.dt.int32
+U32 = mybir.dt.uint32
+U16 = mybir.dt.uint16
+U8 = mybir.dt.uint8
+FP8X4 = mybir.dt.float8_e4m3fn_x4
+FP4X4 = mybir.dt.float4_e2m1fn_x4
+ACT = mybir.ActivationFunctionType
+ALU = mybir.AluOpType
+
+P = 128
+PACK = 4
+N, T, D, NQ, DV = 512, 2048, 1024, 512, 512
+PASSES = D // (P * PACK)
+EPS = 1e-05
+FLOPS = 2 * N * NQ * (D + DV)
+Q_SPLIT = 160
+PARK = 16
+Y_SPLIT = 4
+
+
+def interleave(copy, grouped, planes, c0, c1):
+    copy(
+        out=grouped[:, c0:c1, :].rearrange("p (c i) t -> p c t i", i=4),
+        in_=planes[:, :, c0:c1].rearrange("p t (c i) -> p c t i", i=4),
+    )
+
+
+def tile_attend_atb_relu2_topk_kernel(tc, qT, k_words, k_scales, vT, ts, us, offs, out):
+    nc = tc.nc
+    with ExitStack() as ctx:
+        keep = ctx.enter_context(tc.tile_pool(name="keep", bufs=1))
+        psum = ctx.enter_context(tc.psum_pool(name="psum", bufs=1))
+
+        offsets = keep.tile([P, N // 16], U16, name="offsets")
+        ks_win = keep.tile([P, T], U8, name="ks_win")
+        ts_win = keep.tile([P, T], F32, name="ts_win", tag="slot2")
+        one = keep.tile([P, 1], F32, name="one", tag="slot1")
+        warm = keep.tile([P, 1], F32, name="warm", tag="slot3")
+        ident = keep.tile([P, P], F32, name="ident")
+        k_scale = [keep.tile([P, N], U8, name=f"k_scale{o}", align_bytes=64) for o in range(PASSES)]
+
+        nc.gpsimd.memset(ks_win[:].bitcast(I32), 0)
+        nc.vector.memset(ts_win[:].bitcast(I32), 0)
+        nc.vector.memset(one[:], 1.0)
+        nc.gpsimd.memset(k_scale[1][:].bitcast(I32), 0)
+        make_identity(nc, ident[:])
+
+        def load_q(o, tag):
+            raw = keep.tile([P, PACK, NQ], F32, name=f"q_raw{o}", tag=tag)
+            rows = qT[0, o * P * PACK : (o + 1) * P * PACK, :]
+            nc.sync.dma_start(out=raw[:], in_=rows.rearrange("(p j) w -> p j w", j=PACK))
+            return raw
+
+        def load_v(b):
+            win = keep.tile([P, T], F32, name=f"v_win{b}", tag=f"slot{b}")
+            nc.sync.dma_start(out=win[:], in_=vT[b * P : (b + 1) * P, :])
+            return win
+
+        nc.sync.dma_start(offsets[:], offs)
+        q_raw0 = load_q(0, "slot0")
+        scale_rows = k_scales.rearrange("o (quad j) t -> j quad o t", j=4)
+        for j in range(4):
+            nc.sync.dma_start(out=ks_win[j:P:PARK, :].bitcast(I32), in_=scale_rows[j].bitcast(I32))
+        nc.sync.dma_start(out=ts_win[0:1, :], in_=ts[0:1, :])
+        nc.scalar.activation(out=warm[:], in_=one[:], func=ACT.Abs_reciprocal_sqrt)
+        kw_win = keep.tile([P, T], U32, name="kw_win", tag="slot1")
+        nc.sync.dma_start(
+            out=kw_win[:].bitcast(I32), in_=k_words[0].rearrange("p t b -> p (t b)").bitcast(I32)
+        )
+        q_raw1 = load_q(1, "slot3")
+
+        ks_got = keep.tile([P, N], U8, name="ks_got", tag="small")
+        nc.vector.tensor_copy(out=ks_got[:], in_=ks_win[:].indirect(offsets[:]))
+        nc.vector.tensor_copy(
+            out=k_scale[0][:].rearrange("p (r s) -> p s r", r=PACK),
+            in_=ks_got[:].rearrange("p (s r) -> p s r", r=PACK),
+        )
+        nc.sync.dma_start(
+            out=k_scale[1][0 : P - PARK, :].bitcast(I32), in_=k_scale[0][PARK:P, :].bitcast(I32)
+        )
+        us_col = keep.tile([P, PACK], F32, name="us_col", tag="small")
+        nc.sync.dma_start(out=us_col[:], in_=us[0].rearrange("(s r) o -> s (r o)", r=PACK))
+        ts_got = keep.tile([P, N], F32, name="ts_got")
+        nc.vector.tensor_copy(out=ts_got[:], in_=ts_win[:].indirect(offsets[:]))
+        ts_turned = psum.tile([P, PACK, P], F32, name="ts_turned")
+        for r in range(PACK):
+            nc.tensor.transpose(ts_turned[:, r, :], ts_got[:, r:N:PACK], ident[:])
+        ts_col = keep.tile([P, PACK], F32, name="ts_col")
+        nc.vector.tensor_copy(out=ts_col[:], in_=ts_turned[:, :, 0])
+
+        q_grouped = [keep.tile([P, NQ, PACK], BF16, name=f"q_grouped{o}", align_bytes=64) for o in range(PASSES)]
+        q_codes = [keep.tile([P, NQ], U32, name=f"q_codes{o}", align_bytes=64) for o in range(PASSES)]
+        q_scale = [keep.tile([P, NQ], U8, name=f"q_scale{o}", align_bytes=64) for o in range(PASSES)]
+
+        def quantize_q(o):
+            nc.vector.quantize_mx(
+                out=q_codes[o][:].bitcast(FP8X4),
+                scales=q_scale[o][:],
+                in_=q_grouped[o][:].rearrange("p w j -> p (w j)"),
+            )
+
+        interleave(nc.scalar.copy, q_grouped[0], q_raw0, 0, NQ)
+        v_win = [load_v(0)]
+
+        kw_got = keep.tile([P, N], U32, name="kw_got", tag="slot2")
+        nc.vector.tensor_copy(out=kw_got[:], in_=kw_win[:].indirect(offsets[:]))
+        v_win.append(load_v(1))
+        quantize_q(0)
+        k_codes = [keep.tile([P, N], U16, name=f"k_codes{o}", align_bytes=64) for o in range(PASSES)]
+        kw_halves = kw_got[:].bitcast(U16).rearrange("p (s r o) -> p o s r", r=PACK, o=PASSES)
+        for o in range(PASSES):
+            nc.vector.tensor_copy(
+                out=k_codes[o][:].rearrange("p (r s) -> p s r", r=PACK), in_=kw_halves[:, o]
+            )
+        v_win.append(load_v(2))
+
+        scores = [psum.tile([P, NQ], F32, name=f"scores{r}", tag=f"acc{r}") for r in range(PACK)]
+
+        def score_pass(o):
+            for r in range(PACK):
+                cols = slice(r * P, (r + 1) * P)
+                nc.tensor.matmul_mx(
+                    out=scores[r][:],
+                    lhsT=k_codes[o][:, cols].bitcast(FP4X4),
+                    lhsT_scale=k_scale[o][:, cols],
+                    rhs=q_codes[o][:].bitcast(FP8X4),
+                    rhs_scale=q_scale[o][:],
+                    start=(o == 0),
+                    stop=(o == PASSES - 1),
+                )
+
+        score_pass(0)
+        interleave(nc.scalar.copy, q_grouped[1], q_raw1, 0, Q_SPLIT)
+        interleave(nc.vector.tensor_copy, q_grouped[1], q_raw1, Q_SPLIT, NQ)
+        v_win.append(load_v(3))
+        quantize_q(1)
+        score_pass(1)
+
+        v_codes = keep.tile([P, DV], U32, name="v_codes", align_bytes=64)
+        v_scale = keep.tile([P, DV], U8, name="v_scale", align_bytes=64)
+
+        def gather_v(b, tag):
+            v_got = keep.tile([P, N], BF16, name=f"v_got{b}", tag=tag, align_bytes=64)
+            nc.vector.tensor_copy(out=v_got[:], in_=v_win[b][:].indirect(offsets[:]))
+            words = v_got[:].bitcast(F32)
+            turned = psum.tile([P, 2, P], F32, name=f"v_turned{b}", tag=f"v_turned{b % 2}")
+            for u in range(2):
+                nc.tensor.transpose(turned[:, u, :], words[:, u : N // 2 : 2], ident[:])
+            grouped = keep.tile([P, P, PACK], BF16, name=f"v_grouped{b}", align_bytes=64)
+            nc.scalar.copy(
+                out=grouped[:].rearrange("p e t -> p (e t)").bitcast(F32).rearrange("p (e u) -> p e u", u=2),
+                in_=turned[:].rearrange("p u e -> p e u"),
+            )
+            return grouped
+
+        def quantize_v(b, grouped):
+            cols = slice(b * P, (b + 1) * P)
+            nc.vector.quantize_mx(
+                out=v_codes[:, cols].bitcast(FP8X4),
+                scales=v_scale[:, cols],
+                in_=grouped[:].rearrange("p e t -> p (e t)"),
+            )
+
+        y_planes = keep.tile([P, PACK, NQ], BF16, name="y_planes")
+
+        def weigh(r):
+            relu = keep.tile([P, NQ], F32, name=f"relu{r}", align_bytes=64)
+            nc.scalar.activation(out=relu[:], in_=scores[r][:], func=ACT.Relu, scale=ts_col[:, r : r + 1])
+            nc.vector.scalar_tensor_tensor(
+                out=y_planes[:, r, :], in0=relu[:], scalar=us_col[:, r : r + 1], in1=relu[:],
+                op0=ALU.mult, op1=ALU.mult,
+            )
+
+        y_grouped = keep.tile([P, NQ, PACK], BF16, name="y_grouped", align_bytes=64)
+        y_codes = keep.tile([P, NQ], U32, name="y_codes", align_bytes=64)
+        y_scale = keep.tile([P, NQ], U8, name="y_scale", align_bytes=64)
+        tiles = range(NQ // P)
+        early = DV - P
+        squares = keep.tile([P, early], BF16, name="squares")
+        sq_early = keep.tile([P, NQ // P], F32, name="sq_early")
+        sq_late = keep.tile([P, NQ // P], F32, name="sq_late")
+        ms_early = keep.tile([P, NQ // P], F32, name="ms_early")
+        rstd = keep.tile([P, NQ // P], F32, name="rstd")
+
+        def quantize_y(m):
+            cols = slice(m * P, (m + 1) * P)
+            nc.vector.quantize_mx(
+                out=y_codes[:, cols].bitcast(FP8X4),
+                scales=y_scale[:, cols],
+                in_=y_grouped[:, cols, :].rearrange("p w j -> p (w j)"),
+            )
+
+        g0 = gather_v(0, "v_got0")
+        for r in range(PACK):
+            weigh(r)
+        for m in tiles:
+            interleave(nc.scalar.copy if m < Y_SPLIT else nc.vector.tensor_copy, y_grouped, y_planes, m * P, (m + 1) * P)
+        g1 = gather_v(1, "relu3")
+        g2 = gather_v(2, "v_got2")
+        quantize_v(0, g0)
+        quantize_v(1, g1)
+        for m in tiles:
+            quantize_y(m)
+        quantize_v(2, g2)
+        g3 = gather_v(3, "y_grouped")
+        quantize_v(3, g3)
+
+        sums = [psum.tile([P, DV], F32, name=f"sums{m}", tag=f"acc{m}") for m in tiles]
+
+        def product(m, e0, e1):
+            rows = slice(m * P, (m + 1) * P)
+            nc.tensor.matmul_mx(
+                out=sums[m][:, e0:e1],
+                lhsT=y_codes[:, rows].bitcast(FP8X4),
+                lhsT_scale=y_scale[:, rows],
+                rhs=v_codes[:, e0:e1].bitcast(FP8X4),
+                rhs_scale=v_scale[:, e0:e1],
+                start=True,
+                stop=True,
+            )
+
+        for m in tiles:
+            col = slice(m, m + 1)
+            product(m, 0, 2 * P)
+            product(m, 2 * P, early)
+            nc.scalar.activation(
+                out=squares[:], in_=sums[m][:, 0:early], func=ACT.Square, accum_out=sq_early[:, col]
+            )
+            nc.vector.tensor_scalar(
+                out=ms_early[:, col], in0=sq_early[:, col], scalar1=1.0 / DV, scalar2=EPS,
+                op0=ALU.mult, op1=ALU.add,
+            )
+        for m in tiles:
+            product(m, early, DV)
+        for m in tiles:
+            col = slice(m, m + 1)
+            nc.scalar.activation(
+                out=squares[:, 0:P], in_=sums[m][:, early:DV], func=ACT.Square, accum_out=sq_late[:, col]
+            )
+            nc.scalar.activation(
+                out=rstd[:, col], in_=sq_late[:, col], func=ACT.Abs_reciprocal_sqrt,
+                scale=1.0 / DV, bias=ms_early[:, col],
+            )
+        for m in tiles:
+            col = slice(m, m + 1)
+            result = keep.tile([P, DV], F32, name=f"result{m}")
+            if m < 3:
+                nc.vector.tensor_scalar(
+                    out=result[:], in0=sums[m][:], scalar1=rstd[:, col], scalar2=None, op0=ALU.mult
+                )
+            else:
+                nc.scalar.activation(out=result[:], in_=sums[m][:], func=ACT.Copy, scale=rstd[:, col])
+            nc.sync.dma_start(out=out[0, m * P : (m + 1) * P, :], in_=result[:])

@@ -20,9 +20,8 @@ N, T, D, NQ, DV = 512, 2048, 1024, 512, 512
 PASSES = D // (P * PACK)
 EPS = 1e-05
 FLOPS = 2 * N * NQ * (D + DV)
-Q_SPLIT = 160
+Q_SPLIT = 352
 PARK = 16
-Y_SPLIT = 4
 
 
 def interleave(copy, grouped, planes, c0, c1):
@@ -39,12 +38,16 @@ def tile_attend_atb_relu2_topk_kernel(tc, qT, k_words, k_scales, vT, ts, us, off
         psum = ctx.enter_context(tc.psum_pool(name="psum", bufs=1))
 
         offsets = keep.tile([P, N // 16], U16, name="offsets")
-        ks_win = keep.tile([P, T], U8, name="ks_win")
-        ts_win = keep.tile([P, T], F32, name="ts_win", tag="slot2")
-        one = keep.tile([P, 1], F32, name="one", tag="slot1")
-        warm = keep.tile([P, 1], F32, name="warm", tag="slot3")
-        ident = keep.tile([P, P], F32, name="ident")
-        k_scale = [keep.tile([P, N], U8, name=f"k_scale{o}", align_bytes=64) for o in range(PASSES)]
+
+        def sbuf(shape, dtype, name, tag=None):
+            return keep.tile(shape, dtype, name=name, tag=tag or name, align_bytes=64)
+
+        ks_win = sbuf([P, T], U8, name="ks_win", tag="A")
+        ts_win = sbuf([P, T], F32, name="ts_win", tag="B")
+        one = sbuf([P, 1], F32, name="one", tag="D")
+        warm = sbuf([P, 1], F32, name="warm", tag="E")
+        ident = sbuf([P, P], F32, name="ident")
+        k_scale = [sbuf([P, N], U8, name=f"k_scale{o}") for o in range(PASSES)]
 
         nc.gpsimd.memset(ks_win[:].bitcast(I32), 0)
         nc.vector.memset(ts_win[:].bitcast(I32), 0)
@@ -52,32 +55,39 @@ def tile_attend_atb_relu2_topk_kernel(tc, qT, k_words, k_scales, vT, ts, us, off
         nc.gpsimd.memset(k_scale[1][:].bitcast(I32), 0)
         make_identity(nc, ident[:])
 
-        def load_q(o, tag):
-            raw = keep.tile([P, PACK, NQ], F32, name=f"q_raw{o}", tag=tag)
+        def load_q(o, queue, tag):
+            raw = sbuf([P, PACK, NQ], F32, name=f"q_raw{o}", tag=tag)
             rows = qT[0, o * P * PACK : (o + 1) * P * PACK, :]
-            nc.sync.dma_start(out=raw[:], in_=rows.rearrange("(p j) w -> p j w", j=PACK))
+            queue.dma_start(out=raw[:], in_=rows.rearrange("(p j) w -> p j w", j=PACK))
             return raw
 
-        def load_v(b):
-            win = keep.tile([P, T], F32, name=f"v_win{b}", tag=f"slot{b}")
+        def load_v(b, tag):
+            win = sbuf([P, T], F32, name=f"v_win{b}", tag=tag)
             nc.sync.dma_start(out=win[:], in_=vT[b * P : (b + 1) * P, :])
             return win
 
         nc.sync.dma_start(offsets[:], offs)
-        q_raw0 = load_q(0, "slot0")
+        q_raw0 = load_q(0, nc.sync, "F")
         scale_rows = k_scales.rearrange("o (quad j) t -> j quad o t", j=4)
         for j in range(4):
-            nc.sync.dma_start(out=ks_win[j:P:PARK, :].bitcast(I32), in_=scale_rows[j].bitcast(I32))
+            queue = nc.sync if j < 3 else nc.scalar
+            queue.dma_start(out=ks_win[j:P:PARK, :].bitcast(I32), in_=scale_rows[j].bitcast(I32))
         nc.sync.dma_start(out=ts_win[0:1, :], in_=ts[0:1, :])
         nc.scalar.activation(out=warm[:], in_=one[:], func=ACT.Abs_reciprocal_sqrt)
-        kw_win = keep.tile([P, T], U32, name="kw_win", tag="slot1")
-        nc.sync.dma_start(
+        kw_win = sbuf([P, T], U32, name="kw_win", tag="D")
+        nc.scalar.dma_start(
             out=kw_win[:].bitcast(I32), in_=k_words[0].rearrange("p t b -> p (t b)").bitcast(I32)
         )
-        q_raw1 = load_q(1, "slot3")
+        q_raw1 = load_q(1, nc.scalar, "E")
 
-        ks_got = keep.tile([P, N], U8, name="ks_got", tag="small")
+        q_grouped0 = sbuf([P, NQ, PACK], BF16, name="q_grouped0", tag="G")
+        interleave(nc.scalar.copy, q_grouped0, q_raw0, 0, NQ)
+        us_col = sbuf([P, PACK], F32, name="us_col", tag="F")
+        nc.scalar.dma_start(out=us_col[:], in_=us[0].rearrange("(s r) o -> s (r o)", r=PACK))
+
+        ks_got = sbuf([P, N], U8, name="ks_got", tag="C")
         nc.vector.tensor_copy(out=ks_got[:], in_=ks_win[:].indirect(offsets[:]))
+        v_win = [load_v(0, "A")]
         nc.vector.tensor_copy(
             out=k_scale[0][:].rearrange("p (r s) -> p s r", r=PACK),
             in_=ks_got[:].rearrange("p (s r) -> p s r", r=PACK),
@@ -85,41 +95,39 @@ def tile_attend_atb_relu2_topk_kernel(tc, qT, k_words, k_scales, vT, ts, us, off
         nc.sync.dma_start(
             out=k_scale[1][0 : P - PARK, :].bitcast(I32), in_=k_scale[0][PARK:P, :].bitcast(I32)
         )
-        us_col = keep.tile([P, PACK], F32, name="us_col", tag="small")
-        nc.sync.dma_start(out=us_col[:], in_=us[0].rearrange("(s r) o -> s (r o)", r=PACK))
-        ts_got = keep.tile([P, N], F32, name="ts_got")
+        ts_got = sbuf([P, N], F32, name="ts_got", tag="C")
         nc.vector.tensor_copy(out=ts_got[:], in_=ts_win[:].indirect(offsets[:]))
         ts_turned = psum.tile([P, PACK, P], F32, name="ts_turned")
         for r in range(PACK):
             nc.tensor.transpose(ts_turned[:, r, :], ts_got[:, r:N:PACK], ident[:])
-        ts_col = keep.tile([P, PACK], F32, name="ts_col")
-        nc.vector.tensor_copy(out=ts_col[:], in_=ts_turned[:, :, 0])
+        ts_col = sbuf([P, PACK], F32, name="ts_col")
+        nc.scalar.copy(out=ts_col[:], in_=ts_turned[:, :, 0])
 
-        q_grouped = [keep.tile([P, NQ, PACK], BF16, name=f"q_grouped{o}", align_bytes=64) for o in range(PASSES)]
-        q_codes = [keep.tile([P, NQ], U32, name=f"q_codes{o}", align_bytes=64) for o in range(PASSES)]
-        q_scale = [keep.tile([P, NQ], U8, name=f"q_scale{o}", align_bytes=64) for o in range(PASSES)]
-
-        def quantize_q(o):
-            nc.vector.quantize_mx(
-                out=q_codes[o][:].bitcast(FP8X4),
-                scales=q_scale[o][:],
-                in_=q_grouped[o][:].rearrange("p w j -> p (w j)"),
-            )
-
-        interleave(nc.scalar.copy, q_grouped[0], q_raw0, 0, NQ)
-        v_win = [load_v(0)]
-
-        kw_got = keep.tile([P, N], U32, name="kw_got", tag="slot2")
+        kw_got = sbuf([P, N], U32, name="kw_got", tag="B")
         nc.vector.tensor_copy(out=kw_got[:], in_=kw_win[:].indirect(offsets[:]))
-        v_win.append(load_v(1))
-        quantize_q(0)
-        k_codes = [keep.tile([P, N], U16, name=f"k_codes{o}", align_bytes=64) for o in range(PASSES)]
+        v_win.append(load_v(1, "D"))
+        k_codes = [sbuf([P, N], U16, name=f"k_codes{o}") for o in range(PASSES)]
         kw_halves = kw_got[:].bitcast(U16).rearrange("p (s r o) -> p o s r", r=PACK, o=PASSES)
-        for o in range(PASSES):
+
+        def part_words(o):
             nc.vector.tensor_copy(
                 out=k_codes[o][:].rearrange("p (r s) -> p s r", r=PACK), in_=kw_halves[:, o]
             )
-        v_win.append(load_v(2))
+
+        part_words(0)
+        q_codes = [sbuf([P, NQ], U32, name=f"q_codes{o}") for o in range(PASSES)]
+        q_scale = [sbuf([P, NQ], U8, name=f"q_scale{o}") for o in range(PASSES)]
+
+        def quantize_q(o, grouped):
+            nc.vector.quantize_mx(
+                out=q_codes[o][:].bitcast(FP8X4),
+                scales=q_scale[o][:],
+                in_=grouped[:].rearrange("p w j -> p (w j)"),
+            )
+
+        quantize_q(0, q_grouped0)
+        part_words(1)
+        v_win.append(load_v(2, "B"))
 
         scores = [psum.tile([P, NQ], F32, name=f"scores{r}", tag=f"acc{r}") for r in range(PACK)]
 
@@ -137,23 +145,30 @@ def tile_attend_atb_relu2_topk_kernel(tc, qT, k_words, k_scales, vT, ts, us, off
                 )
 
         score_pass(0)
-        interleave(nc.scalar.copy, q_grouped[1], q_raw1, 0, Q_SPLIT)
-        interleave(nc.vector.tensor_copy, q_grouped[1], q_raw1, Q_SPLIT, NQ)
-        v_win.append(load_v(3))
-        quantize_q(1)
+        q_grouped1 = sbuf([P, NQ, PACK], BF16, name="q_grouped1", tag="G")
+        interleave(nc.scalar.copy, q_grouped1, q_raw1, 0, Q_SPLIT)
+        interleave(nc.vector.tensor_copy, q_grouped1, q_raw1, Q_SPLIT, NQ)
+        v_win.append(load_v(3, "E"))
+        quantize_q(1, q_grouped1)
         score_pass(1)
 
-        v_codes = keep.tile([P, DV], U32, name="v_codes", align_bytes=64)
-        v_scale = keep.tile([P, DV], U8, name="v_scale", align_bytes=64)
+        v_codes = sbuf([P, DV], U32, name="v_codes")
+        v_scale = sbuf([P, DV], U8, name="v_scale")
 
         def gather_v(b, tag):
-            v_got = keep.tile([P, N], BF16, name=f"v_got{b}", tag=tag, align_bytes=64)
+            v_got = sbuf([P, N], BF16, name=f"v_got{b}", tag=tag)
             nc.vector.tensor_copy(out=v_got[:], in_=v_win[b][:].indirect(offsets[:]))
+            return v_got
+
+        def turn_v(b, v_got, bank):
             words = v_got[:].bitcast(F32)
-            turned = psum.tile([P, 2, P], F32, name=f"v_turned{b}", tag=f"v_turned{b % 2}")
+            turned = psum.tile([P, 2, P], F32, name=f"v_turned{b}", tag=bank)
             for u in range(2):
                 nc.tensor.transpose(turned[:, u, :], words[:, u : N // 2 : 2], ident[:])
-            grouped = keep.tile([P, P, PACK], BF16, name=f"v_grouped{b}", align_bytes=64)
+            return turned
+
+        def group_v(b, turned, tag):
+            grouped = sbuf([P, P, PACK], BF16, name=f"v_grouped{b}", tag=tag)
             nc.scalar.copy(
                 out=grouped[:].rearrange("p e t -> p (e t)").bitcast(F32).rearrange("p (e u) -> p e u", u=2),
                 in_=turned[:].rearrange("p u e -> p e u"),
@@ -168,26 +183,26 @@ def tile_attend_atb_relu2_topk_kernel(tc, qT, k_words, k_scales, vT, ts, us, off
                 in_=grouped[:].rearrange("p e t -> p (e t)"),
             )
 
-        y_planes = keep.tile([P, PACK, NQ], BF16, name="y_planes")
+        y_planes = sbuf([P, PACK, NQ], BF16, name="y_planes")
 
         def weigh(r):
-            relu = keep.tile([P, NQ], F32, name=f"relu{r}", align_bytes=64)
+            relu = sbuf([P, NQ], F32, name=f"relu{r}")
             nc.scalar.activation(out=relu[:], in_=scores[r][:], func=ACT.Relu, scale=ts_col[:, r : r + 1])
             nc.vector.scalar_tensor_tensor(
                 out=y_planes[:, r, :], in0=relu[:], scalar=us_col[:, r : r + 1], in1=relu[:],
                 op0=ALU.mult, op1=ALU.mult,
             )
 
-        y_grouped = keep.tile([P, NQ, PACK], BF16, name="y_grouped", align_bytes=64)
-        y_codes = keep.tile([P, NQ], U32, name="y_codes", align_bytes=64)
-        y_scale = keep.tile([P, NQ], U8, name="y_scale", align_bytes=64)
+        y_grouped = sbuf([P, NQ, PACK], BF16, name="y_grouped")
+        y_codes = sbuf([P, NQ], U32, name="y_codes")
+        y_scale = sbuf([P, NQ], U8, name="y_scale")
         tiles = range(NQ // P)
         early = DV - P
-        squares = keep.tile([P, early], BF16, name="squares")
-        sq_early = keep.tile([P, NQ // P], F32, name="sq_early")
-        sq_late = keep.tile([P, NQ // P], F32, name="sq_late")
-        ms_early = keep.tile([P, NQ // P], F32, name="ms_early")
-        rstd = keep.tile([P, NQ // P], F32, name="rstd")
+        squares = sbuf([P, NQ // P, P], BF16, name="squares")
+        sq_early = sbuf([P, NQ // P], F32, name="sq_early")
+        sq_late = sbuf([P, NQ // P], F32, name="sq_late")
+        ms_early = sbuf([P, NQ // P], F32, name="ms_early")
+        rstd = sbuf([P, NQ // P], F32, name="rstd")
 
         def quantize_y(m):
             cols = slice(m * P, (m + 1) * P)
@@ -197,20 +212,20 @@ def tile_attend_atb_relu2_topk_kernel(tc, qT, k_words, k_scales, vT, ts, us, off
                 in_=y_grouped[:, cols, :].rearrange("p w j -> p (w j)"),
             )
 
-        g0 = gather_v(0, "v_got0")
+        got0 = gather_v(0, "G")
         for r in range(PACK):
             weigh(r)
+        g0 = group_v(0, turn_v(0, got0, "acc3"), "v_grouped0")
         for m in tiles:
-            interleave(nc.scalar.copy if m < Y_SPLIT else nc.vector.tensor_copy, y_grouped, y_planes, m * P, (m + 1) * P)
-        g1 = gather_v(1, "relu3")
-        g2 = gather_v(2, "v_got2")
+            interleave(nc.scalar.copy, y_grouped, y_planes, m * P, (m + 1) * P)
+        g1 = group_v(1, turn_v(1, gather_v(1, "relu3"), "turn1"), "v_grouped1")
+        g2 = group_v(2, turn_v(2, gather_v(2, "D"), "turn2"), "v_grouped2")
         quantize_v(0, g0)
         quantize_v(1, g1)
         for m in tiles:
             quantize_y(m)
         quantize_v(2, g2)
-        g3 = gather_v(3, "y_grouped")
-        quantize_v(3, g3)
+        got3 = gather_v(3, "v_grouped2")
 
         sums = [psum.tile([P, DV], F32, name=f"sums{m}", tag=f"acc{m}") for m in tiles]
 
@@ -226,35 +241,58 @@ def tile_attend_atb_relu2_topk_kernel(tc, qT, k_words, k_scales, vT, ts, us, off
                 stop=True,
             )
 
-        for m in tiles:
-            col = slice(m, m + 1)
+        def early_products(m):
             product(m, 0, 2 * P)
             product(m, 2 * P, early)
+
+        def early_squares(m):
+            col = slice(m, m + 1)
+            unused = sbuf([P, early], BF16, name=f"squares_early{m}")
             nc.scalar.activation(
-                out=squares[:], in_=sums[m][:, 0:early], func=ACT.Square, accum_out=sq_early[:, col]
+                out=unused[:], in_=sums[m][:, 0:early], func=ACT.Square, accum_out=sq_early[:, col]
             )
             nc.vector.tensor_scalar(
                 out=ms_early[:, col], in0=sq_early[:, col], scalar1=1.0 / DV, scalar2=EPS,
                 op0=ALU.mult, op1=ALU.add,
             )
+
         for m in tiles:
-            product(m, early, DV)
-        for m in tiles:
+            early_products(m)
+        turned3 = turn_v(3, got3, "turn1")
+
+        def late_squares(m):
             col = slice(m, m + 1)
             nc.scalar.activation(
-                out=squares[:, 0:P], in_=sums[m][:, early:DV], func=ACT.Square, accum_out=sq_late[:, col]
+                out=squares[:, m, :], in_=sums[m][:, early:DV], func=ACT.Square, accum_out=sq_late[:, col]
             )
             nc.scalar.activation(
                 out=rstd[:, col], in_=sq_late[:, col], func=ACT.Abs_reciprocal_sqrt,
                 scale=1.0 / DV, bias=ms_early[:, col],
             )
-        for m in tiles:
+
+        def store(m):
             col = slice(m, m + 1)
-            result = keep.tile([P, DV], F32, name=f"result{m}")
-            if m < 3:
+            result = sbuf([P, DV], F32, name=f"result{m}")
+            rows = out[0, m * P : (m + 1) * P, :]
+            if m < tiles[-1]:
                 nc.vector.tensor_scalar(
                     out=result[:], in0=sums[m][:], scalar1=rstd[:, col], scalar2=None, op0=ALU.mult
                 )
+                nc.sync.dma_start(out=rows, in_=result[:])
             else:
                 nc.scalar.activation(out=result[:], in_=sums[m][:], func=ACT.Copy, scale=rstd[:, col])
-            nc.sync.dma_start(out=out[0, m * P : (m + 1) * P, :], in_=result[:])
+                nc.scalar.dma_start(out=rows, in_=result[:])
+
+        early_squares(0)
+        early_squares(1)
+        quantize_v(3, group_v(3, turned3, "squares_early1"))
+        early_squares(2)
+        for m in (0, 1):
+            product(m, early, DV)
+            late_squares(m)
+            store(m)
+        early_squares(3)
+        for m in (2, 3):
+            product(m, early, DV)
+            late_squares(m)
+            store(m)

from contextlib import ExitStack

import concourse.mybir as mybir
from concourse.masks import make_identity

F32 = mybir.dt.float32
BF16 = mybir.dt.bfloat16
I32 = mybir.dt.int32
U32 = mybir.dt.uint32
U16 = mybir.dt.uint16
U8 = mybir.dt.uint8
FP8X4 = mybir.dt.float8_e4m3fn_x4
FP4X4 = mybir.dt.float4_e2m1fn_x4
ACT = mybir.ActivationFunctionType
ALU = mybir.AluOpType

P = 128
PACK = 4
N, T, D, NQ, DV = 512, 2048, 1024, 512, 512
PASSES = D // (P * PACK)
EPS = 1e-05
FLOPS = 2 * N * NQ * (D + DV)
Q_SPLIT = 352
PARK = 16


def interleave(copy, grouped, planes, c0, c1):
    copy(
        out=grouped[:, c0:c1, :].rearrange("p (c i) t -> p c t i", i=4),
        in_=planes[:, :, c0:c1].rearrange("p t (c i) -> p c t i", i=4),
    )


def tile_attend_atb_relu2_topk_kernel(tc, qT, k_words, k_scales, vT, ts, us, offs, out):
    nc = tc.nc
    with ExitStack() as ctx:
        keep = ctx.enter_context(tc.tile_pool(name="keep", bufs=1))
        psum = ctx.enter_context(tc.psum_pool(name="psum", bufs=1))

        offsets = keep.tile([P, N // 16], U16, name="offsets")

        def sbuf(shape, dtype, name, tag=None):
            return keep.tile(shape, dtype, name=name, tag=tag or name, align_bytes=64)

        ks_win = sbuf([P, T], U8, name="ks_win", tag="A")
        ts_win = sbuf([P, T], F32, name="ts_win", tag="B")
        one = sbuf([P, 1], F32, name="one", tag="D")
        warm = sbuf([P, 1], F32, name="warm", tag="E")
        ident = sbuf([P, P], F32, name="ident")
        k_scale = [sbuf([P, N], U8, name=f"k_scale{o}") for o in range(PASSES)]

        nc.gpsimd.memset(ks_win[:].bitcast(I32), 0)
        nc.vector.memset(ts_win[:].bitcast(I32), 0)
        nc.vector.memset(one[:], 1.0)
        nc.gpsimd.memset(k_scale[1][:].bitcast(I32), 0)
        make_identity(nc, ident[:])

        def load_q(o, queue, tag):
            raw = sbuf([P, PACK, NQ], F32, name=f"q_raw{o}", tag=tag)
            rows = qT[0, o * P * PACK : (o + 1) * P * PACK, :]
            queue.dma_start(out=raw[:], in_=rows.rearrange("(p j) w -> p j w", j=PACK))
            return raw

        def load_v(b, tag):
            win = sbuf([P, T], F32, name=f"v_win{b}", tag=tag)
            nc.sync.dma_start(out=win[:], in_=vT[b * P : (b + 1) * P, :])
            return win

        nc.sync.dma_start(offsets[:], offs)
        q_raw0 = load_q(0, nc.sync, "F")
        scale_rows = k_scales.rearrange("o (quad j) t -> j quad o t", j=4)
        for j in range(4):
            queue = nc.sync if j < 3 else nc.scalar
            queue.dma_start(out=ks_win[j:P:PARK, :].bitcast(I32), in_=scale_rows[j].bitcast(I32))
        nc.sync.dma_start(out=ts_win[0:1, :], in_=ts[0:1, :])
        nc.scalar.activation(out=warm[:], in_=one[:], func=ACT.Abs_reciprocal_sqrt)
        kw_win = sbuf([P, T], U32, name="kw_win", tag="D")
        nc.scalar.dma_start(
            out=kw_win[:].bitcast(I32), in_=k_words[0].rearrange("p t b -> p (t b)").bitcast(I32)
        )
        q_raw1 = load_q(1, nc.scalar, "E")

        q_grouped0 = sbuf([P, NQ, PACK], BF16, name="q_grouped0", tag="G")
        interleave(nc.scalar.copy, q_grouped0, q_raw0, 0, NQ)
        us_col = sbuf([P, PACK], F32, name="us_col", tag="F")
        nc.scalar.dma_start(out=us_col[:], in_=us[0].rearrange("(s r) o -> s (r o)", r=PACK))

        ks_got = sbuf([P, N], U8, name="ks_got", tag="C")
        nc.vector.tensor_copy(out=ks_got[:], in_=ks_win[:].indirect(offsets[:]))
        v_win = [load_v(0, "A")]
        nc.vector.tensor_copy(
            out=k_scale[0][:].rearrange("p (r s) -> p s r", r=PACK),
            in_=ks_got[:].rearrange("p (s r) -> p s r", r=PACK),
        )
        nc.sync.dma_start(
            out=k_scale[1][0 : P - PARK, :].bitcast(I32), in_=k_scale[0][PARK:P, :].bitcast(I32)
        )
        ts_got = sbuf([P, N], F32, name="ts_got", tag="C")
        nc.vector.tensor_copy(out=ts_got[:], in_=ts_win[:].indirect(offsets[:]))
        ts_turned = psum.tile([P, PACK, P], F32, name="ts_turned")
        for r in range(PACK):
            nc.tensor.transpose(ts_turned[:, r, :], ts_got[:, r:N:PACK], ident[:])
        ts_col = sbuf([P, PACK], F32, name="ts_col")
        nc.scalar.copy(out=ts_col[:], in_=ts_turned[:, :, 0])

        kw_got = sbuf([P, N], U32, name="kw_got", tag="B")
        nc.vector.tensor_copy(out=kw_got[:], in_=kw_win[:].indirect(offsets[:]))
        v_win.append(load_v(1, "D"))
        k_codes = [sbuf([P, N], U16, name=f"k_codes{o}") for o in range(PASSES)]
        kw_halves = kw_got[:].bitcast(U16).rearrange("p (s r o) -> p o s r", r=PACK, o=PASSES)

        def part_words(o):
            nc.vector.tensor_copy(
                out=k_codes[o][:].rearrange("p (r s) -> p s r", r=PACK), in_=kw_halves[:, o]
            )

        part_words(0)
        q_codes = [sbuf([P, NQ], U32, name=f"q_codes{o}") for o in range(PASSES)]
        q_scale = [sbuf([P, NQ], U8, name=f"q_scale{o}") for o in range(PASSES)]

        def quantize_q(o, grouped):
            nc.vector.quantize_mx(
                out=q_codes[o][:].bitcast(FP8X4),
                scales=q_scale[o][:],
                in_=grouped[:].rearrange("p w j -> p (w j)"),
            )

        quantize_q(0, q_grouped0)
        part_words(1)
        v_win.append(load_v(2, "B"))

        scores = [psum.tile([P, NQ], F32, name=f"scores{r}", tag=f"acc{r}") for r in range(PACK)]

        def score_pass(o):
            for r in range(PACK):
                cols = slice(r * P, (r + 1) * P)
                nc.tensor.matmul_mx(
                    out=scores[r][:],
                    lhsT=k_codes[o][:, cols].bitcast(FP4X4),
                    lhsT_scale=k_scale[o][:, cols],
                    rhs=q_codes[o][:].bitcast(FP8X4),
                    rhs_scale=q_scale[o][:],
                    start=(o == 0),
                    stop=(o == PASSES - 1),
                )

        score_pass(0)
        q_grouped1 = sbuf([P, NQ, PACK], BF16, name="q_grouped1", tag="G")
        interleave(nc.scalar.copy, q_grouped1, q_raw1, 0, Q_SPLIT)
        interleave(nc.vector.tensor_copy, q_grouped1, q_raw1, Q_SPLIT, NQ)
        v_win.append(load_v(3, "E"))
        quantize_q(1, q_grouped1)
        score_pass(1)

        v_codes = sbuf([P, DV], U32, name="v_codes")
        v_scale = sbuf([P, DV], U8, name="v_scale")

        def gather_v(b, tag):
            v_got = sbuf([P, N], BF16, name=f"v_got{b}", tag=tag)
            nc.vector.tensor_copy(out=v_got[:], in_=v_win[b][:].indirect(offsets[:]))
            return v_got

        def turn_v(b, v_got, bank):
            words = v_got[:].bitcast(F32)
            turned = psum.tile([P, 2, P], F32, name=f"v_turned{b}", tag=bank)
            for u in range(2):
                nc.tensor.transpose(turned[:, u, :], words[:, u : N // 2 : 2], ident[:])
            return turned

        def group_v(b, turned, tag):
            grouped = sbuf([P, P, PACK], BF16, name=f"v_grouped{b}", tag=tag)
            nc.scalar.copy(
                out=grouped[:].rearrange("p e t -> p (e t)").bitcast(F32).rearrange("p (e u) -> p e u", u=2),
                in_=turned[:].rearrange("p u e -> p e u"),
            )
            return grouped

        def quantize_v(b, grouped):
            cols = slice(b * P, (b + 1) * P)
            nc.vector.quantize_mx(
                out=v_codes[:, cols].bitcast(FP8X4),
                scales=v_scale[:, cols],
                in_=grouped[:].rearrange("p e t -> p (e t)"),
            )

        y_planes = sbuf([P, PACK, NQ], BF16, name="y_planes")

        def weigh(r):
            relu = sbuf([P, NQ], F32, name=f"relu{r}")
            nc.scalar.activation(out=relu[:], in_=scores[r][:], func=ACT.Relu, scale=ts_col[:, r : r + 1])
            nc.vector.scalar_tensor_tensor(
                out=y_planes[:, r, :], in0=relu[:], scalar=us_col[:, r : r + 1], in1=relu[:],
                op0=ALU.mult, op1=ALU.mult,
            )

        y_grouped = sbuf([P, NQ, PACK], BF16, name="y_grouped")
        y_codes = sbuf([P, NQ], U32, name="y_codes")
        y_scale = sbuf([P, NQ], U8, name="y_scale")
        tiles = range(NQ // P)
        early = DV - P
        squares = sbuf([P, NQ // P, P], BF16, name="squares")
        sq_early = sbuf([P, NQ // P], F32, name="sq_early")
        sq_late = sbuf([P, NQ // P], F32, name="sq_late")
        ms_early = sbuf([P, NQ // P], F32, name="ms_early")
        rstd = sbuf([P, NQ // P], F32, name="rstd")

        def quantize_y(m):
            cols = slice(m * P, (m + 1) * P)
            nc.vector.quantize_mx(
                out=y_codes[:, cols].bitcast(FP8X4),
                scales=y_scale[:, cols],
                in_=y_grouped[:, cols, :].rearrange("p w j -> p (w j)"),
            )

        got0 = gather_v(0, "G")
        for r in range(PACK):
            weigh(r)
        g0 = group_v(0, turn_v(0, got0, "acc3"), "v_grouped0")
        for m in tiles:
            interleave(nc.scalar.copy, y_grouped, y_planes, m * P, (m + 1) * P)
        g1 = group_v(1, turn_v(1, gather_v(1, "relu3"), "turn1"), "v_grouped1")
        g2 = group_v(2, turn_v(2, gather_v(2, "D"), "turn2"), "v_grouped2")
        quantize_v(0, g0)
        quantize_v(1, g1)
        for m in tiles:
            quantize_y(m)
        quantize_v(2, g2)
        got3 = gather_v(3, "v_grouped2")

        sums = [psum.tile([P, DV], F32, name=f"sums{m}", tag=f"acc{m}") for m in tiles]

        def product(m, e0, e1):
            rows = slice(m * P, (m + 1) * P)
            nc.tensor.matmul_mx(
                out=sums[m][:, e0:e1],
                lhsT=y_codes[:, rows].bitcast(FP8X4),
                lhsT_scale=y_scale[:, rows],
                rhs=v_codes[:, e0:e1].bitcast(FP8X4),
                rhs_scale=v_scale[:, e0:e1],
                start=True,
                stop=True,
            )

        def early_products(m):
            product(m, 0, 2 * P)
            product(m, 2 * P, early)

        def early_squares(m):
            col = slice(m, m + 1)
            unused = sbuf([P, early], BF16, name=f"squares_early{m}")
            nc.scalar.activation(
                out=unused[:], in_=sums[m][:, 0:early], func=ACT.Square, accum_out=sq_early[:, col]
            )
            nc.vector.tensor_scalar(
                out=ms_early[:, col], in0=sq_early[:, col], scalar1=1.0 / DV, scalar2=EPS,
                op0=ALU.mult, op1=ALU.add,
            )

        for m in tiles:
            early_products(m)
        turned3 = turn_v(3, got3, "turn1")

        def late_squares(m):
            col = slice(m, m + 1)
            nc.scalar.activation(
                out=squares[:, m, :], in_=sums[m][:, early:DV], func=ACT.Square, accum_out=sq_late[:, col]
            )
            nc.scalar.activation(
                out=rstd[:, col], in_=sq_late[:, col], func=ACT.Abs_reciprocal_sqrt,
                scale=1.0 / DV, bias=ms_early[:, col],
            )

        def store(m):
            col = slice(m, m + 1)
            result = sbuf([P, DV], F32, name=f"result{m}")
            rows = out[0, m * P : (m + 1) * P, :]
            if m < tiles[-1]:
                nc.vector.tensor_scalar(
                    out=result[:], in0=sums[m][:], scalar1=rstd[:, col], scalar2=None, op0=ALU.mult
                )
                nc.sync.dma_start(out=rows, in_=result[:])
            else:
                nc.scalar.activation(out=result[:], in_=sums[m][:], func=ACT.Copy, scale=rstd[:, col])
                nc.scalar.dma_start(out=rows, in_=result[:])

        early_squares(0)
        early_squares(1)
        quantize_v(3, group_v(3, turned3, "squares_early1"))
        early_squares(2)
        for m in (0, 1):
            product(m, early, DV)
            late_squares(m)
            store(m)
        early_squares(3)
        for m in (2, 3):
            product(m, early, DV)
            late_squares(m)
            store(m)
